import numpy as np
import ml_dtypes


def mxq(x, axis, fmt="e4m3"):
    dtype, down = {"e4m3": (ml_dtypes.float8_e4m3fn, 7), "e5m2": (ml_dtypes.float8_e5m2, 14)}[fmt]
    v = np.moveaxis(np.asarray(x, np.float32).astype(ml_dtypes.bfloat16).astype(np.float64), axis, -1)
    blocks = v.reshape(v.shape[:-1] + (-1, 32))
    amax = np.abs(blocks).max(-1, keepdims=True)
    byte = np.maximum(np.where(amax > 0, np.frexp(amax)[1] - 1 + 127, 0) - down, 1)
    scale = np.exp2(byte - 127.0)
    codes = (blocks / scale).astype(np.float32).astype(dtype).astype(np.float64)
    return np.moveaxis((codes * scale).reshape(v.shape), -1, axis)


WIDE = False


def mx_kscale(k):
    if not WIDE:
        return np.ones(k)
    levels = np.array([10, -10, 5, -5, 0])
    if k % 512:
        return np.exp2(np.random.permutation(np.resize(levels, k // 32))).repeat(32)
    a = np.empty((k // 512, 16))
    for p in range(k // 512):
        a[p, :8] = np.random.permutation(np.resize(levels, 8))
        for g in range(8):
            far = levels[np.abs(levels - a[p, g]) >= 10]
            a[p, g + 8] = far[np.random.randint(len(far))]
    return np.exp2(a.ravel()).repeat(32)


def f64(x):
    return np.asarray(x).astype(np.float64)


def striped(idx):
    return np.tile(idx.reshape(-1, 16).T, (8, 1)).astype(np.uint16)


def unstriped(offs):
    return offs[:16].T.reshape(-1).astype(np.int64)


E2M1 = np.array([0.0, 0.5, 1.0, 1.5, 2.0, 3.0, 4.0, 6.0, -0.0, -0.5, -1.0, -1.5, -2.0, -3.0, -4.0, -6.0])


def pack_weight(w, fmt):
    k, n = w.shape
    w = f64(np.asarray(w, np.float32).astype(ml_dtypes.bfloat16)).reshape(k // 32, 32, n)
    amax = np.abs(w).max(1)
    if fmt == "e4m3":
        byte = np.frexp(amax)[1] - 1 + 127 - 7
    else:
        mant, ex = np.frexp(amax / 6.0)
        byte = np.where(mant > 0.5, ex, ex - 1) + 127
    byte = np.clip(np.where(amax > 0, byte, 1), 1, 254)
    scaled = (w * np.exp2(127.0 - byte)[:, None, :]).reshape(k, n).astype(np.float32)
    by_word = np.ascontiguousarray(scaled.reshape(k // 512, 128, 4, n).transpose(0, 1, 3, 2))
    if fmt == "e4m3":
        words = by_word.astype(ml_dtypes.float8_e4m3fn).view(np.uint8)
    else:
        c = by_word.astype(ml_dtypes.float4_e2m1fn).view(np.uint8) & 0xF
        words = (c[..., 0::2] | (c[..., 1::2] << 4)).reshape(k // 512, 128, 2 * n)
    return np.ascontiguousarray(words), np.ascontiguousarray(byte.astype(np.uint8).reshape(k // 512, 16, n))


def unpack_weight(words, scales, fmt):
    g, _, n = scales.shape
    words = np.ascontiguousarray(words).reshape(g, 128, n, -1)
    if fmt == "e4m3":
        vals = words.view(ml_dtypes.float8_e4m3fn).astype(np.float64)
    else:
        nib = np.empty((g, 128, n, 4), np.uint8)
        nib[..., 0::2] = words & 0xF
        nib[..., 1::2] = words >> 4
        vals = E2M1[nib]
    vals = vals * np.repeat(np.exp2(scales.astype(np.float64) - 127.0), 8, axis=1)[..., None]
    return vals.transpose(0, 1, 3, 2).reshape(g * 512, n)


def gelu(v):
    return 0.5 * v * (1.0 + np.tanh(np.sqrt(2.0 / np.pi) * (v + 0.044715 * v**3)))


def striped8(idx):
    return np.concatenate([v.reshape(-1, 16).T for v in idx]).astype(np.uint16)


def unstriped8(offs):
    return np.stack([offs[16 * g:16 * g + 16].T.reshape(-1) for g in range(8)]).astype(np.int64)


def heads(h, wgt, idx8):
    r = np.arange(h.shape[0])
    return wgt[r // 4 % 128] * h[r[:, None], idx8[r % 512 // 64]]


def bf(x):
    return np.asarray(x, np.float32).astype(ml_dtypes.bfloat16)


def planes(Y):
    n, m = Y.shape
    b = f64(bf(Y)).reshape(n // 32, 32, m)
    amax = np.abs(b).max(1)
    byte = np.clip(np.where(amax > 0, np.frexp(amax)[1] - 1 + 127 - 7, 1), 1, 254)
    codes = (b * np.exp2(127.0 - byte)[:, None, :]).reshape(n, m).astype(np.float32).astype(ml_dtypes.float8_e4m3fn).view(np.uint8)
    words = codes.reshape(n // 512, 128, 4, m).transpose(0, 1, 3, 2)
    return np.ascontiguousarray(words), np.ascontiguousarray(byte.astype(np.uint8).reshape(n // 512, 16, m))


K, H, N, T, S, P = 1024, 1024, 512, 4096, 1024, 512

def setup_inputs():
    n = np.random.standard_normal
    s = mx_kscale(K)[:, None]
    u = mx_kscale(H)[:, None]
    tab_words, tab_scales = pack_weight(n((K, T)) * s, "e4m3")
    w1_words, w1_scales = pack_weight(1.4 * n((K, H)) / np.sqrt(K) / s, "e2m1")
    gain = np.exp(0.3 * n(H)) * np.sqrt(u[:, 0])
    w2 = n((H, N)) / np.sqrt(H) / u * np.exp(0.8 * n(N))[None, :]
    wga = np.repeat(np.random.uniform(0.5, 2.0, (8, P)), 16, axis=0)
    wgb = np.repeat(np.random.uniform(0.5, 2.0, (8, P)), 16, axis=0)
    return {
        "tab_words": tab_words, "tab_scales": tab_scales,
        "offs": striped(np.random.permutation(T)[:S]),
        "offs2": striped8(np.stack([np.random.permutation(S)[:P] for _ in range(8)])),
        "offs3": striped8(np.stack([np.random.permutation(S)[:P] for _ in range(8)])),
        "w1_words": w1_words, "w1_scales": w1_scales,
        "gain": gain.astype(np.float32),
        "wga": wga.astype(np.float32), "wgb": wgb.astype(np.float32),
        "w2": w2.astype(np.float32),
    }

def reference(tab_words, tab_scales, offs, offs2, offs3, w1_words, w1_scales, gain, wga, wgb, w2):
    v = unpack_weight(tab_words, tab_scales, "e4m3")[:, unstriped(offs)]
    w1 = unpack_weight(w1_words, w1_scales, "e2m1")
    h = f64(gain)[:, None] * np.tanh(w1.T @ v)
    xa = heads(h, f64(wga), unstriped8(offs2))
    xb = heads(h, f64(wgb), unstriped8(offs3))
    z = xa * xb
    y = mxq(f64(w2), 0, "e4m3").T @ mxq(z, 0, "e4m3")
    words, scales = planes(y)
    return y, words, scales

@@ -1,0 +1,277 @@
+from contextlib import ExitStack
+
+import concourse.mybir as mybir
+
+K, H, N, T, S, M = 1024, 1024, 512, 4096, 1024, 512
+FLOPS = 2 * K * H * S + 2 * H * N * M
+
+F32 = mybir.dt.float32
+BF16 = mybir.dt.bfloat16
+I32 = mybir.dt.int32
+U32 = mybir.dt.uint32
+U16 = mybir.dt.uint16
+U8 = mybir.dt.uint8
+FP8X4 = mybir.dt.float8_e4m3fn_x4
+FP4X4 = mybir.dt.float4_e2m1fn_x4
+MULT = mybir.AluOpType.mult
+TANH = mybir.ActivationFunctionType.Tanh
+COPY = mybir.ActivationFunctionType.Copy
+
+P = 128
+PACK = 4
+HALF = 512
+CHUNK = 128
+CHUNKS = M // CHUNK
+SLICES = H // P
+VECTOR_GAINS = 2
+
+
+def tile_list_coral_neighbour_features_kernel(
+    tc, tab_words, tab_scales, offs, offs2, offs3, w1_words, w1_scales, gain, wga, wgb, w2, out_0, out_1, out_2
+):
+    nc = tc.nc
+    with ExitStack() as ctx:
+        held = ctx.enter_context(tc.tile_pool(name="held", bufs=1))
+        ring = ctx.enter_context(tc.tile_pool(name="ring", bufs=3))
+        hbanks = ctx.enter_context(tc.psum_pool(name="hbanks", bufs=4))
+        ybanks = ctx.enter_context(tc.psum_pool(name="ybanks", bufs=1))
+
+        idx = held.tile([P, S // 16], U16, name="idx")
+        idx2 = held.tile([P, M // 16], U16, name="idx2")
+        idx3 = held.tile([P, M // 16], U16, name="idx3")
+        tab_w = [held.tile([P, T], U32, name=f"tab_w{a}", align_bytes=64) for a in range(2)]
+        tab_s = held.tile([P, T], U8, name="tab_s", align_bytes=64)
+        v_w = [held.tile([P, S], U32, name=f"v_w{a}", align_bytes=64) for a in range(2)]
+        v_s = [held.tile([P, S], U8, name=f"v_s{a}", align_bytes=64) for a in range(2)]
+        w1_raw = held.tile([P, 2 * H], U16, name="w1_raw", align_bytes=64)
+        w1s_raw = held.tile([P, 2 * H], U8, name="w1s_raw", align_bytes=64)
+        w1_w = [held.tile([P, H], U16, name=f"w1_w{a}", align_bytes=64) for a in range(2)]
+        w1_s = [held.tile([P, H], U8, name=f"w1_s{a}", align_bytes=64) for a in range(2)]
+        gains = held.tile([P, SLICES], F32, name="gains")
+        wa = held.tile([P, M], F32, name="wa")
+        wb = held.tile([P, M], F32, name="wb")
+        wab = held.tile([P, M], F32, name="wab")
+        w2_raw = held.tile([P, 2, PACK, N], F32, name="w2_raw")
+        w2_bf = [held.tile([P, N * PACK], BF16, name=f"w2_bf{b}", align_bytes=64) for b in range(2)]
+        w2_w = [held.tile([P, N], U32, name=f"w2_w{b}", align_bytes=64) for b in range(2)]
+        w2_s = [held.tile([P, N], U8, name=f"w2_s{b}", align_bytes=64) for b in range(2)]
+        h = [held.tile([P, S], F32, name=f"h{s}", align_bytes=64) for s in range(SLICES)]
+        z = [held.tile([P, PACK, M], F32, name=f"z{b}", align_bytes=64) for b in range(2)]
+        z_bf = [held.tile([P, M * PACK], BF16, name=f"z_bf{b}", align_bytes=64) for b in range(2)]
+        z_w = [held.tile([P, M], U32, name=f"z_w{b}", align_bytes=64) for b in range(2)]
+        z_s = [held.tile([P, M], U8, name=f"z_s{b}", align_bytes=64) for b in range(2)]
+        y = [held.tile([P, PACK, CHUNK], F32, name=f"y{c}", align_bytes=64) for c in range(CHUNKS)]
+        y_bf = [held.tile([P, CHUNK * PACK], BF16, name=f"y_bf{c}", align_bytes=64) for c in range(CHUNKS)]
+        y_w = held.tile([P, M], U32, name="y_w", align_bytes=64)
+        y_s = held.tile([P, M], U8, name="y_s", align_bytes=64)
+        y_bank = [ybanks.tile([P, PACK, CHUNK], F32, name=f"y_bank{c}") for c in range(CHUNKS)]
+
+        nc.vector.memset(tab_s[:].bitcast(I32), 0)
+        nc.gpsimd.memset(w1s_raw[:].bitcast(I32), 0)
+        nc.gpsimd.memset(v_s[1][:].bitcast(I32), 0)
+        nc.sync.dma_start(idx[:], offs)
+        nc.sync.dma_start(
+            w1_raw[:].bitcast(I32).rearrange("p (a c) -> p a c", a=2),
+            w1_words.bitcast(I32).rearrange("a p c -> p a c"),
+        )
+        for q in range(4):
+            nc.sync.dma_start(
+                tab_s[32 * q : 32 * q + 8, :].bitcast(I32), tab_scales[:, 4 * q : 4 * q + 4, :].bitcast(I32)
+            )
+        nc.sync.dma_start(tab_w[0][:].bitcast(I32), tab_words[0].rearrange("p t i -> p (t i)").bitcast(I32))
+        for q in range(4):
+            nc.sync.dma_start(
+                w1s_raw[32 * q : 32 * q + 4, :].bitcast(I32).rearrange("r (a c) -> r a c", a=2),
+                w1_scales[:, 4 * q : 4 * q + 4, :].bitcast(I32).rearrange("a r c -> r a c"),
+            )
+        nc.sync.dma_start(tab_w[1][:].bitcast(I32), tab_words[1].rearrange("p t i -> p (t i)").bitcast(I32))
+        nc.sync.dma_start(idx2[:], offs2)
+        nc.sync.dma_start(idx3[:], offs3)
+        nc.sync.dma_start(wa[:], wga)
+        nc.sync.dma_start(wb[:], wgb)
+        nc.sync.dma_start(
+            gains[:].rearrange("p (b i) -> p b i", b=2), gain.rearrange("(b p i) -> p b i", b=2, i=PACK)
+        )
+        nc.sync.dma_start(
+            w2_raw[:].rearrange("p b j n -> p b (j n)"), w2.rearrange("(b p j) n -> p b (j n)", b=2, j=PACK)
+        )
+
+        def deal(dst, src):
+            nc.vector.tensor_copy(
+                dst.rearrange("p (b i q) -> p b i q", b=2, i=PACK), src.rearrange("p (b q i) -> p b i q", b=2, i=PACK)
+            )
+
+        for a in range(2):
+            deal(w1_w[a][:], w1_raw[:, a * H : (a + 1) * H])
+        nc.vector.tensor_copy(v_s[0][:], tab_s[:].indirect(idx[:]))
+        nc.scalar.dma_start(v_s[1][0:100, :].bitcast(I32), v_s[0][4:104, :].bitcast(I32))
+        nc.vector.tensor_copy(v_w[0][:], tab_w[0][:].indirect(idx[:]))
+        for a in range(2):
+            deal(w1_s[a][:], w1s_raw[:, a * H : (a + 1) * H])
+
+        banks = {}
+        tanhs = {}
+
+        def first_product(s, half, a):
+            if a == 0:
+                banks[s, half] = hbanks.tile([P, HALF], F32, name="h_bank")
+            rows = slice(s * P, (s + 1) * P)
+            cols = slice(half * HALF, (half + 1) * HALF)
+            nc.tensor.matmul_mx(
+                out=banks[s, half][:],
+                lhsT=w1_w[a][:, rows].bitcast(FP4X4),
+                lhsT_scale=w1_s[a][:, rows],
+                rhs=v_w[a][:, cols].bitcast(FP8X4),
+                rhs_scale=v_s[a][:, cols],
+                start=(a == 0),
+                stop=(a == 1),
+            )
+
+        def tanh(s, half):
+            if half == 0:
+                tanhs[s] = ring.tile([P, S], F32, name="tanh")
+            nc.scalar.activation(tanhs[s][:, half * HALF : (half + 1) * HALF], banks[s, half][:], TANH)
+
+        def apply_gain(s, cols):
+            if s < VECTOR_GAINS:
+                nc.vector.tensor_scalar(h[s][:, cols], tanhs[s][:, cols], gains[:, s : s + 1], None, MULT)
+            else:
+                nc.scalar.activation(h[s][:, cols], tanhs[s][:, cols], COPY, scale=gains[:, s : s + 1])
+
+        lefts = {}
+
+        def pick_left(s, m0, m1):
+            lefts[s, m0] = ring.tile([P, m1 - m0], F32, name="left")
+            nc.vector.tensor_tensor(
+                lefts[s, m0][:], h[s][:].indirect(idx2[:, m0 // 16 : m1 // 16]), wab[:, m0:m1], MULT
+            )
+
+        def pick_right(s, m0, m1, l0):
+            nc.vector.tensor_tensor(
+                z[s // PACK][:, s % PACK, m0:m1],
+                h[s][:].indirect(idx3[:, m0 // 16 : m1 // 16]),
+                lefts[s, l0][:, m0 - l0 : m1 - l0],
+                MULT,
+            )
+
+        def weave(engine_copy, dst, src):
+            engine_copy(
+                dst.rearrange("p (c i t) -> p c t i", i=4, t=PACK), src.rearrange("p t (c i) -> p c t i", i=4)
+            )
+
+        def round_w2(b):
+            nc.scalar.copy(
+                w2_bf[b][:].rearrange("p (t q j) -> p q j t", t=PACK, j=PACK),
+                w2_raw[:, b].rearrange("p j (q t) -> p q j t", t=PACK),
+            )
+
+        def quantize(words, scales, rounded, m0, m1):
+            nc.vector.quantize_mx(
+                out=words[:, m0:m1].bitcast(FP8X4), scales=scales[:, m0:m1], in_=rounded
+            )
+
+        def second_product(c, b):
+            cols = slice(c * CHUNK, (c + 1) * CHUNK)
+            for t in range(PACK):
+                rows = slice(t * P, (t + 1) * P)
+                nc.tensor.matmul_mx(
+                    out=y_bank[c][:, t, :],
+                    lhsT=w2_w[b][:, rows].bitcast(FP8X4),
+                    lhsT_scale=w2_s[b][:, rows],
+                    rhs=z_w[b][:, cols].bitcast(FP8X4),
+                    rhs_scale=z_s[b][:, cols],
+                    start=(b == 0 and t == 0),
+                    stop=(b == 1 and t == PACK - 1),
+                )
+
+        out_rows = out_0.rearrange("(p t) m -> p t m", t=PACK)
+        out_words = out_1[0].rearrange("p m t -> p (m t)").bitcast(I32)
+
+        def round_z(c, engine_copy):
+            m0, m1 = c * CHUNK, (c + 1) * CHUNK
+            weave(engine_copy, z_bf[1][:, m0 * PACK : m1 * PACK], z[1][:, :, m0:m1])
+
+        def multiply(c):
+            m0, m1 = c * CHUNK, (c + 1) * CHUNK
+            quantize(z_w[1], z_s[1], z_bf[1][:, m0 * PACK : m1 * PACK], m0, m1)
+            second_product(c, 1)
+
+        def drain(c, engine_copy):
+            m0, m1 = c * CHUNK, (c + 1) * CHUNK
+            nc.scalar.copy(y[c][:], y_bank[c][:])
+            nc.sync.dma_start(out_rows[:, :, m0:m1], y[c][:])
+            weave(engine_copy, y_bf[c][:], y[c][:])
+
+        def planes(c):
+            m0, m1 = c * CHUNK, (c + 1) * CHUNK
+            quantize(y_w, y_s, y_bf[c][:], m0, m1)
+            nc.sync.dma_start(out_words[:, m0:m1], y_w[:, m0:m1].bitcast(I32))
+
+        for s in range(2):
+            for half in range(2):
+                first_product(s, half, 0)
+        for half in range(2):
+            cols = slice(half * HALF, (half + 1) * HALF)
+            nc.vector.tensor_copy(v_w[1][:, cols], tab_w[1][:].indirect(idx[:, half * 32 : (half + 1) * 32]))
+        for half in range(2):
+            for s in range(2):
+                first_product(s, half, 1)
+                tanh(s, half)
+        nc.vector.tensor_tensor(wab[:], wa[:], wb[:], MULT)
+        for half in range(2):
+            apply_gain(0, slice(half * HALF, (half + 1) * HALF))
+        pick_left(0, 0, M)
+        apply_gain(1, slice(0, S))
+
+        def make_h(s):
+            for half in range(2):
+                for a in range(2):
+                    first_product(s, half, a)
+                tanh(s, half)
+            apply_gain(s, slice(0, S))
+
+        for s in range(1, 6):
+            make_h(s + 1)
+            if s == 3:
+                round_w2(0)
+            pick_left(s, 0, M)
+            pick_right(s - 1, 0, M, 0)
+            if s == 4:
+                weave(nc.vector.tensor_copy, z_bf[0][:], z[0][:])
+                quantize(w2_w[0], w2_s[0], w2_bf[0][:], 0, N)
+            if s == 5:
+                quantize(z_w[0], z_s[0], z_bf[0][:], 0, M)
+                for c in range(CHUNKS):
+                    second_product(c, 0)
+        make_h(7)
+        round_w2(1)
+        pick_left(6, 0, 256)
+        pick_right(5, 0, M, 0)
+        pick_left(7, 0, 256)
+        pick_right(6, 0, 256, 0)
+        pick_left(6, 256, M)
+        pick_right(7, 0, 256, 0)
+        quantize(w2_w[1], w2_s[1], w2_bf[1][:], 0, N)
+        round_z(0, nc.scalar.copy)
+        round_z(1, nc.scalar.copy)
+        pick_left(7, 256, M)
+        pick_right(6, 256, M, 256)
+        multiply(0)
+        pick_right(7, 256, 384, 256)
+        multiply(1)
+        round_z(2, nc.scalar.copy)
+        pick_right(7, 384, M, 256)
+        drain(0, nc.scalar.copy)
+        multiply(2)
+        round_z(3, nc.vector.tensor_copy)
+        drain(1, nc.vector.tensor_copy)
+        multiply(3)
+        planes(0)
+        drain(2, nc.vector.tensor_copy)
+        planes(1)
+        drain(3, nc.vector.tensor_copy)
+        planes(2)
+        planes(3)
+        for q in range(4):
+            queue = nc.sync if q % 2 == 0 else nc.scalar
+            queue.dma_start(out_2[0, 4 * q : 4 * q + 4, :].bitcast(I32), y_s[32 * q : 32 * q + 4, :].bitcast(I32))

@@ -66,9 +66,9 @@ def tile_list_coral_neighbour_features_kernel(
         y_s = held.tile([P, M], U8, name="y_s", align_bytes=64)
         y_bank = [ybanks.tile([P, PACK, CHUNK], F32, name=f"y_bank{c}") for c in range(CHUNKS)]
 
+        nc.vector.memset(w1s_raw[:].bitcast(I32), 0)
         nc.vector.memset(tab_s[:].bitcast(I32), 0)
-        nc.gpsimd.memset(w1s_raw[:].bitcast(I32), 0)
-        nc.gpsimd.memset(v_s[1][:].bitcast(I32), 0)
+        nc.vector.memset(v_s[1][:].bitcast(I32), 0)
         nc.sync.dma_start(idx[:], offs)
         nc.sync.dma_start(
             w1_raw[:].bitcast(I32).rearrange("p (a c) -> p a c", a=2),
@@ -76,15 +76,15 @@ def tile_list_coral_neighbour_features_kernel(
         )
         for q in range(4):
             nc.sync.dma_start(
-                tab_s[32 * q : 32 * q + 8, :].bitcast(I32), tab_scales[:, 4 * q : 4 * q + 4, :].bitcast(I32)
-            )
-        nc.sync.dma_start(tab_w[0][:].bitcast(I32), tab_words[0].rearrange("p t i -> p (t i)").bitcast(I32))
-        for q in range(4):
-            nc.sync.dma_start(
                 w1s_raw[32 * q : 32 * q + 4, :].bitcast(I32).rearrange("r (a c) -> r a c", a=2),
                 w1_scales[:, 4 * q : 4 * q + 4, :].bitcast(I32).rearrange("a r c -> r a c"),
             )
-        nc.sync.dma_start(tab_w[1][:].bitcast(I32), tab_words[1].rearrange("p t i -> p (t i)").bitcast(I32))
+        for q in range(4):
+            nc.gpsimd.dma_start(
+                tab_s[32 * q : 32 * q + 8, :].bitcast(I32), tab_scales[:, 4 * q : 4 * q + 4, :].bitcast(I32)
+            )
+        for a in range(2):
+            nc.sync.dma_start(tab_w[a][:].bitcast(I32), tab_words[a].rearrange("p t i -> p (t i)").bitcast(I32))
         nc.sync.dma_start(idx2[:], offs2)
         nc.sync.dma_start(idx3[:], offs3)
         nc.sync.dma_start(wa[:], wga)
@@ -103,11 +103,11 @@ def tile_list_coral_neighbour_features_kernel(
 
         for a in range(2):
             deal(w1_w[a][:], w1_raw[:, a * H : (a + 1) * H])
+        for a in range(2):
+            deal(w1_s[a][:], w1s_raw[:, a * H : (a + 1) * H])
         nc.vector.tensor_copy(v_s[0][:], tab_s[:].indirect(idx[:]))
         nc.scalar.dma_start(v_s[1][0:100, :].bitcast(I32), v_s[0][4:104, :].bitcast(I32))
         nc.vector.tensor_copy(v_w[0][:], tab_w[0][:].indirect(idx[:]))
-        for a in range(2):
-            deal(w1_s[a][:], w1s_raw[:, a * H : (a + 1) * H])
 
         banks = {}
         tanhs = {}
@@ -156,13 +156,13 @@ def tile_list_coral_neighbour_features_kernel(
 
         def weave(engine_copy, dst, src):
             engine_copy(
-                dst.rearrange("p (c i t) -> p c t i", i=4, t=PACK), src.rearrange("p t (c i) -> p c t i", i=4)
+                dst.rearrange("p (m t) -> p m t", t=PACK), src.rearrange("p t m -> p m t")
             )
 
         def round_w2(b):
             nc.scalar.copy(
-                w2_bf[b][:].rearrange("p (t q j) -> p q j t", t=PACK, j=PACK),
-                w2_raw[:, b].rearrange("p j (q t) -> p q j t", t=PACK),
+                w2_bf[b][:].rearrange("p (t q j) -> p q t j", t=PACK, j=PACK),
+                w2_raw[:, b].rearrange("p j (q t) -> p q t j", t=PACK),
             )
 
         def quantize(words, scales, rounded, m0, m1):

@@ -23,7 +23,7 @@ HALF = 512
 CHUNK = 128
 CHUNKS = M // CHUNK
 SLICES = H // P
-VECTOR_GAINS = 2
+VECTOR_GAINS = 3
 
 
 def tile_list_coral_neighbour_features_kernel(
@@ -32,6 +32,7 @@ def tile_list_coral_neighbour_features_kernel(
     nc = tc.nc
     with ExitStack() as ctx:
         held = ctx.enter_context(tc.tile_pool(name="held", bufs=1))
+        stage = ctx.enter_context(tc.tile_pool(name="stage", bufs=1))
         ring = ctx.enter_context(tc.tile_pool(name="ring", bufs=3))
         hbanks = ctx.enter_context(tc.psum_pool(name="hbanks", bufs=4))
         ybanks = ctx.enter_context(tc.psum_pool(name="ybanks", bufs=1))
@@ -39,19 +40,22 @@ def tile_list_coral_neighbour_features_kernel(
         idx = held.tile([P, S // 16], U16, name="idx")
         idx2 = held.tile([P, M // 16], U16, name="idx2")
         idx3 = held.tile([P, M // 16], U16, name="idx3")
-        tab_w = [held.tile([P, T], U32, name=f"tab_w{a}", align_bytes=64) for a in range(2)]
         tab_s = held.tile([P, T], U8, name="tab_s", align_bytes=64)
+        tab_w = [stage.tile([P, T], U32, name=f"tab_w{a}", align_bytes=64, offset=24576 * a) for a in range(2)]
         v_w = [held.tile([P, S], U32, name=f"v_w{a}", align_bytes=64) for a in range(2)]
         v_s = [held.tile([P, S], U8, name=f"v_s{a}", align_bytes=64) for a in range(2)]
-        w1_raw = held.tile([P, 2 * H], U16, name="w1_raw", align_bytes=64)
+        w1_raw = [
+            held.tile([P, H], U16, name="w1_raw0", align_bytes=64),
+            stage.tile([P, H], U16, name="w1_raw1", align_bytes=64, offset=4096),
+        ]
         w1s_raw = held.tile([P, 2 * H], U8, name="w1s_raw", align_bytes=64)
         w1_w = [held.tile([P, H], U16, name=f"w1_w{a}", align_bytes=64) for a in range(2)]
         w1_s = [held.tile([P, H], U8, name=f"w1_s{a}", align_bytes=64) for a in range(2)]
         gains = held.tile([P, SLICES], F32, name="gains")
-        wa = held.tile([P, M], F32, name="wa")
-        wb = held.tile([P, M], F32, name="wb")
+        wa = stage.tile([P, M], F32, name="wa", offset=0)
+        wb = stage.tile([P, M], F32, name="wb", offset=2048)
         wab = held.tile([P, M], F32, name="wab")
-        w2_raw = held.tile([P, 2, PACK, N], F32, name="w2_raw")
+        w2_raw = stage.tile([P, 2, PACK, N], F32, name="w2_raw", offset=8192)
         w2_bf = [held.tile([P, N * PACK], BF16, name=f"w2_bf{b}", align_bytes=64) for b in range(2)]
         w2_w = [held.tile([P, N], U32, name=f"w2_w{b}", align_bytes=64) for b in range(2)]
         w2_s = [held.tile([P, N], U8, name=f"w2_s{b}", align_bytes=64) for b in range(2)]
@@ -60,77 +64,95 @@ def tile_list_coral_neighbour_features_kernel(
         z_bf = [held.tile([P, M * PACK], BF16, name=f"z_bf{b}", align_bytes=64) for b in range(2)]
         z_w = [held.tile([P, M], U32, name=f"z_w{b}", align_bytes=64) for b in range(2)]
         z_s = [held.tile([P, M], U8, name=f"z_s{b}", align_bytes=64) for b in range(2)]
-        y = [held.tile([P, PACK, CHUNK], F32, name=f"y{c}", align_bytes=64) for c in range(CHUNKS)]
-        y_bf = [held.tile([P, CHUNK * PACK], BF16, name=f"y_bf{c}", align_bytes=64) for c in range(CHUNKS)]
+        y = held.tile([P, PACK, M], F32, name="y", align_bytes=64)
+        y_bf = held.tile([P, M * PACK], BF16, name="y_bf", align_bytes=64)
         y_w = held.tile([P, M], U32, name="y_w", align_bytes=64)
         y_s = held.tile([P, M], U8, name="y_s", align_bytes=64)
         y_bank = [ybanks.tile([P, PACK, CHUNK], F32, name=f"y_bank{c}") for c in range(CHUNKS)]
 
+        nc.vector.memset(tab_s[:].bitcast(I32)[:, :768], 0)
+        nc.gpsimd.memset(tab_s[:].bitcast(I32)[:, 768:], 0)
         nc.vector.memset(w1s_raw[:].bitcast(I32), 0)
-        nc.vector.memset(tab_s[:].bitcast(I32), 0)
         nc.vector.memset(v_s[1][:].bitcast(I32), 0)
-        nc.sync.dma_start(idx[:], offs)
-        nc.sync.dma_start(
-            w1_raw[:].bitcast(I32).rearrange("p (a c) -> p a c", a=2),
-            w1_words.bitcast(I32).rearrange("a p c -> p a c"),
+        nc.gpsimd.dma_start(
+            gains[:].rearrange("p (b i) -> p b i", b=2), gain.rearrange("(b p i) -> p b i", b=2, i=PACK)
         )
+        nc.sync.dma_start(idx[:], offs)
+
+        def load_w1_words(b):
+            nc.sync.dma_start(
+                w1_raw[b][:].bitcast(I32).rearrange("p (a c) -> p a c", a=2),
+                w1_words[:, :, b * H : (b + 1) * H].bitcast(I32).rearrange("a p c -> p a c"),
+            )
+
+        load_w1_words(0)
+        nc.sync.dma_start(tab_s[4:P:8, :].bitcast(I32), tab_scales[1].bitcast(I32))
+        for q in range(4):
+            nc.sync.dma_start(
+                tab_s[32 * q : 32 * q + 4, :].bitcast(I32), tab_scales[0, 4 * q : 4 * q + 4, :].bitcast(I32)
+            )
+
+        def load_table(a):
+            nc.sync.dma_start(tab_w[a][:].bitcast(I32), tab_words[a].rearrange("p t i -> p (t i)").bitcast(I32))
+
+        load_table(0)
         for q in range(4):
             nc.sync.dma_start(
                 w1s_raw[32 * q : 32 * q + 4, :].bitcast(I32).rearrange("r (a c) -> r a c", a=2),
                 w1_scales[:, 4 * q : 4 * q + 4, :].bitcast(I32).rearrange("a r c -> r a c"),
             )
-        for q in range(4):
-            nc.gpsimd.dma_start(
-                tab_s[32 * q : 32 * q + 8, :].bitcast(I32), tab_scales[:, 4 * q : 4 * q + 4, :].bitcast(I32)
-            )
-        for a in range(2):
-            nc.sync.dma_start(tab_w[a][:].bitcast(I32), tab_words[a].rearrange("p t i -> p (t i)").bitcast(I32))
         nc.sync.dma_start(idx2[:], offs2)
         nc.sync.dma_start(idx3[:], offs3)
-        nc.sync.dma_start(wa[:], wga)
-        nc.sync.dma_start(wb[:], wgb)
-        nc.sync.dma_start(
-            gains[:].rearrange("p (b i) -> p b i", b=2), gain.rearrange("(b p i) -> p b i", b=2, i=PACK)
-        )
-        nc.sync.dma_start(
-            w2_raw[:].rearrange("p b j n -> p b (j n)"), w2.rearrange("(b p j) n -> p b (j n)", b=2, j=PACK)
-        )
+        load_table(1)
 
         def deal(dst, src):
             nc.vector.tensor_copy(
-                dst.rearrange("p (b i q) -> p b i q", b=2, i=PACK), src.rearrange("p (b q i) -> p b i q", b=2, i=PACK)
+                dst.rearrange("p (a i q) -> p a i q", a=2, i=PACK), src.rearrange("p a (q i) -> p a i q", i=PACK)
             )
 
-        for a in range(2):
-            deal(w1_w[a][:], w1_raw[:, a * H : (a + 1) * H])
-        for a in range(2):
-            deal(w1_s[a][:], w1s_raw[:, a * H : (a + 1) * H])
+        def deal_words(b):
+            deal(w1_w[b][:], w1_raw[b][:].rearrange("p (a c) -> p a c", a=2))
+
+        def deal_scales(b):
+            deal(w1_s[b][:], w1s_raw[:].rearrange("p (a c) -> p a c", a=2)[:, :, b * HALF : (b + 1) * HALF])
+
         nc.vector.tensor_copy(v_s[0][:], tab_s[:].indirect(idx[:]))
-        nc.scalar.dma_start(v_s[1][0:100, :].bitcast(I32), v_s[0][4:104, :].bitcast(I32))
+        for r in range(4):
+            nc.sync.dma_start(v_s[1][r:P:32, :].bitcast(I32), v_s[0][4 + 8 * r : P : 32, :].bitcast(I32))
+        deal_words(0)
         nc.vector.tensor_copy(v_w[0][:], tab_w[0][:].indirect(idx[:]))
+        nc.sync.dma_start(wa[:], wga)
+        nc.sync.dma_start(wb[:], wgb)
+        load_w1_words(1)
+        nc.sync.dma_start(
+            w2_raw[:].rearrange("p b j n -> p b (j n)"), w2.rearrange("(b p j) n -> p b (j n)", b=2, j=PACK)
+        )
+        deal_scales(0)
+        deal_scales(1)
 
         banks = {}
         tanhs = {}
 
-        def first_product(s, half, a):
+        def first_product(s, j0, j1, a):
             if a == 0:
-                banks[s, half] = hbanks.tile([P, HALF], F32, name="h_bank")
-            rows = slice(s * P, (s + 1) * P)
-            cols = slice(half * HALF, (half + 1) * HALF)
+                banks[s, j0] = hbanks.tile([P, j1 - j0], F32, name="h_bank")
+            b, i = divmod(s, PACK)
+            rows = slice((a * PACK + i) * P, (a * PACK + i + 1) * P)
+            cols = slice(j0, j1)
             nc.tensor.matmul_mx(
-                out=banks[s, half][:],
-                lhsT=w1_w[a][:, rows].bitcast(FP4X4),
-                lhsT_scale=w1_s[a][:, rows],
+                out=banks[s, j0][:],
+                lhsT=w1_w[b][:, rows].bitcast(FP4X4),
+                lhsT_scale=w1_s[b][:, rows],
                 rhs=v_w[a][:, cols].bitcast(FP8X4),
                 rhs_scale=v_s[a][:, cols],
                 start=(a == 0),
                 stop=(a == 1),
             )
 
-        def tanh(s, half):
-            if half == 0:
+        def tanh(s, j0, j1):
+            if j0 == 0:
                 tanhs[s] = ring.tile([P, S], F32, name="tanh")
-            nc.scalar.activation(tanhs[s][:, half * HALF : (half + 1) * HALF], banks[s, half][:], TANH)
+            nc.scalar.activation(tanhs[s][:, j0:j1], banks[s, j0][:], TANH)
 
         def apply_gain(s, cols):
             if s < VECTOR_GAINS:
@@ -170,18 +192,28 @@ def tile_list_coral_neighbour_features_kernel(
                 out=words[:, m0:m1].bitcast(FP8X4), scales=scales[:, m0:m1], in_=rounded
             )
 
+        spare = {}
+
+        def y_sums(c, t):
+            if c == CHUNKS - 1 and t >= 2:
+                return spare[c][:, t - 2, :]
+            return y_bank[c][:, t, :]
+
         def second_product(c, b):
             cols = slice(c * CHUNK, (c + 1) * CHUNK)
+            split = c == CHUNKS - 1
+            if split and b == 0:
+                spare[c] = hbanks.tile([P, 2, CHUNK], F32, name="h_bank")
             for t in range(PACK):
                 rows = slice(t * P, (t + 1) * P)
                 nc.tensor.matmul_mx(
-                    out=y_bank[c][:, t, :],
+                    out=y_sums(c, t),
                     lhsT=w2_w[b][:, rows].bitcast(FP8X4),
                     lhsT_scale=w2_s[b][:, rows],
                     rhs=z_w[b][:, cols].bitcast(FP8X4),
                     rhs_scale=z_s[b][:, cols],
-                    start=(b == 0 and t == 0),
-                    stop=(b == 1 and t == PACK - 1),
+                    start=(b == 0 and (t == 0 or (split and t == 2))),
+                    stop=(b == 1 and (t == PACK - 1 or (split and t == 1))),
                 )
 
         out_rows = out_0.rearrange("(p t) m -> p t m", t=PACK)
@@ -196,82 +228,97 @@ def tile_list_coral_neighbour_features_kernel(
             quantize(z_w[1], z_s[1], z_bf[1][:, m0 * PACK : m1 * PACK], m0, m1)
             second_product(c, 1)
 
-        def drain(c, engine_copy):
-            m0, m1 = c * CHUNK, (c + 1) * CHUNK
-            nc.scalar.copy(y[c][:], y_bank[c][:])
-            nc.sync.dma_start(out_rows[:, :, m0:m1], y[c][:])
-            weave(engine_copy, y_bf[c][:], y[c][:])
+        def drain(c):
+            nc.scalar.copy(y[:, :, c * CHUNK : (c + 1) * CHUNK], y_bank[c][:])
 
-        def planes(c):
-            m0, m1 = c * CHUNK, (c + 1) * CHUNK
-            quantize(y_w, y_s, y_bf[c][:], m0, m1)
+        def store_y(m0, m1):
+            nc.sync.dma_start(out_rows[:, :, m0:m1], y[:, :, m0:m1])
+
+        def round_y(m0, m1, engine_copy):
+            weave(engine_copy, y_bf[:, m0 * PACK : m1 * PACK], y[:, :, m0:m1])
+
+        def quantize_y(m0, m1):
+            quantize(y_w, y_s, y_bf[:, m0 * PACK : m1 * PACK], m0, m1)
+
+        def store_words(m0, m1):
             nc.sync.dma_start(out_words[:, m0:m1], y_w[:, m0:m1].bitcast(I32))
 
-        for s in range(2):
-            for half in range(2):
-                first_product(s, half, 0)
+        early = [(0, 0, HALF), (1, 0, HALF), (0, HALF, 768), (0, 768, S)]
+        for piece in early:
+            first_product(*piece, 0)
         for half in range(2):
             cols = slice(half * HALF, (half + 1) * HALF)
             nc.vector.tensor_copy(v_w[1][:, cols], tab_w[1][:].indirect(idx[:, half * 32 : (half + 1) * 32]))
-        for half in range(2):
-            for s in range(2):
-                first_product(s, half, 1)
-                tanh(s, half)
+        for piece in early:
+            first_product(*piece, 1)
+            tanh(*piece)
         nc.vector.tensor_tensor(wab[:], wa[:], wb[:], MULT)
-        for half in range(2):
-            apply_gain(0, slice(half * HALF, (half + 1) * HALF))
+        for s, j0, j1 in early:
+            if s == 0:
+                apply_gain(s, slice(j0, j1))
         pick_left(0, 0, M)
-        apply_gain(1, slice(0, S))
+        deal_words(1)
 
-        def make_h(s):
-            for half in range(2):
-                for a in range(2):
-                    first_product(s, half, a)
-                tanh(s, half)
+        def make_tanh(s, half):
+            for a in range(2):
+                first_product(s, half * HALF, (half + 1) * HALF, a)
+            tanh(s, half * HALF, (half + 1) * HALF)
+
+        make_tanh(1, 1)
+        for s in range(1, SLICES):
+            if s + 1 < SLICES:
+                make_tanh(s + 1, 0)
             apply_gain(s, slice(0, S))
-
-        for s in range(1, 6):
-            make_h(s + 1)
-            if s == 3:
+            if s == 5:
                 round_w2(0)
-            pick_left(s, 0, M)
-            pick_right(s - 1, 0, M, 0)
+            if s + 1 < SLICES:
+                make_tanh(s + 1, 1)
+            if s < 6:
+                pick_left(s, 0, M)
+                pick_right(s - 1, 0, M, 0)
             if s == 4:
                 weave(nc.vector.tensor_copy, z_bf[0][:], z[0][:])
-                quantize(w2_w[0], w2_s[0], w2_bf[0][:], 0, N)
             if s == 5:
                 quantize(z_w[0], z_s[0], z_bf[0][:], 0, M)
-                for c in range(CHUNKS):
-                    second_product(c, 0)
-        make_h(7)
         round_w2(1)
         pick_left(6, 0, 256)
         pick_right(5, 0, M, 0)
+        quantize(w2_w[0], w2_s[0], w2_bf[0][:], 0, N)
+        for c in range(CHUNKS):
+            second_product(c, 0)
         pick_left(7, 0, 256)
         pick_right(6, 0, 256, 0)
         pick_left(6, 256, M)
         pick_right(7, 0, 256, 0)
-        quantize(w2_w[1], w2_s[1], w2_bf[1][:], 0, N)
         round_z(0, nc.scalar.copy)
         round_z(1, nc.scalar.copy)
         pick_left(7, 256, M)
-        pick_right(6, 256, M, 256)
+        quantize(w2_w[1], w2_s[1], w2_bf[1][:], 0, N)
+        pick_right(6, 256, 384, 256)
         multiply(0)
         pick_right(7, 256, 384, 256)
-        multiply(1)
         round_z(2, nc.scalar.copy)
+        multiply(1)
+        pick_right(6, 384, M, 256)
         pick_right(7, 384, M, 256)
-        drain(0, nc.scalar.copy)
+        drain(0)
         multiply(2)
         round_z(3, nc.vector.tensor_copy)
-        drain(1, nc.vector.tensor_copy)
+        drain(1)
+        store_y(0, 256)
         multiply(3)
-        planes(0)
-        drain(2, nc.vector.tensor_copy)
-        planes(1)
-        drain(3, nc.vector.tensor_copy)
-        planes(2)
-        planes(3)
+        round_y(0, 256, nc.vector.tensor_copy)
+        drain(2)
+        store_y(256, 384)
+        quantize_y(0, 256)
+        store_words(0, 256)
+        nc.scalar.copy(y[:, 0:2, 384:M], y_bank[3][:, 0:2, :])
+        nc.vector.tensor_copy(y[:, 2:4, 384:M], spare[3][:])
+        store_y(384, M)
+        round_y(256, 384, nc.scalar.copy)
+        round_y(384, M, nc.vector.tensor_copy)
+        quantize_y(256, M)
+        store_words(256, M)
         for q in range(4):
             queue = nc.sync if q % 2 == 0 else nc.scalar
             queue.dma_start(out_2[0, 4 * q : 4 * q + 4, :].bitcast(I32), y_s[32 * q : 32 * q + 4, :].bitcast(I32))

@@ -19,11 +19,23 @@ COPY = mybir.ActivationFunctionType.Copy
 
 P = 128
 PACK = 4
-HALF = 512
+PASSES = 2
+PASS_ROWS = P * PACK
+QUADRANT = 32
+QUADRANTS = P // QUADRANT
+LIST_ROWS = 16
+SLICES = H // P
+BANK = 512
+QUARTER = BANK // 2
 CHUNK = 128
 CHUNKS = M // CHUNK
-SLICES = H // P
+LAST = CHUNKS - 1
+MID = M // 2
+LAST_M0 = LAST * CHUNK
 VECTOR_GAINS = 3
+WHOLE_SLICES = SLICES - 2
+VECTOR_CLEARS = 768
+WA_AT, WB_AT, W1_AT, W2_AT, TABLE_STEP = 0, 2048, 4096, 8192, 24576
 
 
 def tile_list_coral_neighbour_features_kernel(
@@ -37,149 +49,157 @@ def tile_list_coral_neighbour_features_kernel(
         hbanks = ctx.enter_context(tc.psum_pool(name="hbanks", bufs=4))
         ybanks = ctx.enter_context(tc.psum_pool(name="ybanks", bufs=1))
 
-        idx = held.tile([P, S // 16], U16, name="idx")
-        idx2 = held.tile([P, M // 16], U16, name="idx2")
-        idx3 = held.tile([P, M // 16], U16, name="idx3")
+        idx = held.tile([P, S // LIST_ROWS], U16, name="idx")
+        idx2 = held.tile([P, M // LIST_ROWS], U16, name="idx2")
+        idx3 = held.tile([P, M // LIST_ROWS], U16, name="idx3")
         tab_s = held.tile([P, T], U8, name="tab_s", align_bytes=64)
-        tab_w = [stage.tile([P, T], U32, name=f"tab_w{a}", align_bytes=64, offset=24576 * a) for a in range(2)]
-        v_w = [held.tile([P, S], U32, name=f"v_w{a}", align_bytes=64) for a in range(2)]
-        v_s = [held.tile([P, S], U8, name=f"v_s{a}", align_bytes=64) for a in range(2)]
+        tab_w = [
+            stage.tile([P, T], U32, name=f"tab_w{a}", align_bytes=64, offset=TABLE_STEP * a) for a in range(PASSES)
+        ]
+        v_w = [held.tile([P, S], U32, name=f"v_w{a}", align_bytes=64) for a in range(PASSES)]
+        v_s = [held.tile([P, S], U8, name=f"v_s{a}", align_bytes=64) for a in range(PASSES)]
         w1_raw = [
             held.tile([P, H], U16, name="w1_raw0", align_bytes=64),
-            stage.tile([P, H], U16, name="w1_raw1", align_bytes=64, offset=4096),
+            stage.tile([P, H], U16, name="w1_raw1", align_bytes=64, offset=W1_AT),
         ]
-        w1s_raw = held.tile([P, 2 * H], U8, name="w1s_raw", align_bytes=64)
-        w1_w = [held.tile([P, H], U16, name=f"w1_w{a}", align_bytes=64) for a in range(2)]
-        w1_s = [held.tile([P, H], U8, name=f"w1_s{a}", align_bytes=64) for a in range(2)]
+        w1s_raw = held.tile([P, PASSES * H], U8, name="w1s_raw", align_bytes=64)
+        w1_w = [held.tile([P, H], U16, name=f"w1_w{b}", align_bytes=64) for b in range(PASSES)]
+        w1_s = [held.tile([P, H], U8, name=f"w1_s{b}", align_bytes=64) for b in range(PASSES)]
         gains = held.tile([P, SLICES], F32, name="gains")
-        wa = stage.tile([P, M], F32, name="wa", offset=0)
-        wb = stage.tile([P, M], F32, name="wb", offset=2048)
+        wa = stage.tile([P, M], F32, name="wa", offset=WA_AT)
+        wb = stage.tile([P, M], F32, name="wb", offset=WB_AT)
         wab = held.tile([P, M], F32, name="wab")
-        w2_raw = stage.tile([P, 2, PACK, N], F32, name="w2_raw", offset=8192)
-        w2_bf = [held.tile([P, N * PACK], BF16, name=f"w2_bf{b}", align_bytes=64) for b in range(2)]
-        w2_w = [held.tile([P, N], U32, name=f"w2_w{b}", align_bytes=64) for b in range(2)]
-        w2_s = [held.tile([P, N], U8, name=f"w2_s{b}", align_bytes=64) for b in range(2)]
+        w2_raw = stage.tile([P, PASSES, PACK, N], F32, name="w2_raw", offset=W2_AT)
+        w2_bf = [held.tile([P, N * PACK], BF16, name=f"w2_bf{b}", align_bytes=64) for b in range(PASSES)]
+        w2_w = [held.tile([P, N], U32, name=f"w2_w{b}", align_bytes=64) for b in range(PASSES)]
+        w2_s = [held.tile([P, N], U8, name=f"w2_s{b}", align_bytes=64) for b in range(PASSES)]
         h = [held.tile([P, S], F32, name=f"h{s}", align_bytes=64) for s in range(SLICES)]
-        z = [held.tile([P, PACK, M], F32, name=f"z{b}", align_bytes=64) for b in range(2)]
-        z_bf = [held.tile([P, M * PACK], BF16, name=f"z_bf{b}", align_bytes=64) for b in range(2)]
-        z_w = [held.tile([P, M], U32, name=f"z_w{b}", align_bytes=64) for b in range(2)]
-        z_s = [held.tile([P, M], U8, name=f"z_s{b}", align_bytes=64) for b in range(2)]
+        z_all = held.tile([P, SLICES, M], F32, name="z_all", align_bytes=64)
+        z = [z_all[:, b * PACK : (b + 1) * PACK, :] for b in range(PASSES)]
+        z_bf = [held.tile([P, M * PACK], BF16, name=f"z_bf{b}", align_bytes=64) for b in range(PASSES)]
+        z_w = [held.tile([P, M], U32, name=f"z_w{b}", align_bytes=64) for b in range(PASSES)]
+        z_s = [held.tile([P, M], U8, name=f"z_s{b}", align_bytes=64) for b in range(PASSES)]
         y = held.tile([P, PACK, M], F32, name="y", align_bytes=64)
         y_bf = held.tile([P, M * PACK], BF16, name="y_bf", align_bytes=64)
         y_w = held.tile([P, M], U32, name="y_w", align_bytes=64)
         y_s = held.tile([P, M], U8, name="y_s", align_bytes=64)
         y_bank = [ybanks.tile([P, PACK, CHUNK], F32, name=f"y_bank{c}") for c in range(CHUNKS)]
 
-        nc.vector.memset(tab_s[:].bitcast(I32)[:, :768], 0)
-        nc.gpsimd.memset(tab_s[:].bitcast(I32)[:, 768:], 0)
-        nc.vector.memset(w1s_raw[:].bitcast(I32), 0)
-        nc.vector.memset(v_s[1][:].bitcast(I32), 0)
-        nc.gpsimd.dma_start(
-            gains[:].rearrange("p (b i) -> p b i", b=2), gain.rearrange("(b p i) -> p b i", b=2, i=PACK)
-        )
-        nc.sync.dma_start(idx[:], offs)
+        def scale_rows(tile, q):
+            return tile[QUADRANT * q : QUADRANT * q + PACK, :].bitcast(I32)
 
         def load_w1_words(b):
             nc.sync.dma_start(
-                w1_raw[b][:].bitcast(I32).rearrange("p (a c) -> p a c", a=2),
+                w1_raw[b][:].bitcast(I32).rearrange("p (a c) -> p a c", a=PASSES),
                 w1_words[:, :, b * H : (b + 1) * H].bitcast(I32).rearrange("a p c -> p a c"),
-            )
-
-        load_w1_words(0)
-        nc.sync.dma_start(tab_s[4:P:8, :].bitcast(I32), tab_scales[1].bitcast(I32))
-        for q in range(4):
-            nc.sync.dma_start(
-                tab_s[32 * q : 32 * q + 4, :].bitcast(I32), tab_scales[0, 4 * q : 4 * q + 4, :].bitcast(I32)
             )
 
         def load_table(a):
             nc.sync.dma_start(tab_w[a][:].bitcast(I32), tab_words[a].rearrange("p t i -> p (t i)").bitcast(I32))
 
+        def deal(dst, src):
+            nc.vector.tensor_copy(
+                dst.rearrange("p (a i q) -> p a i q", a=PASSES, i=PACK),
+                src.rearrange("p a (q i) -> p a i q", i=PACK),
+            )
+
+        def deal_words(b):
+            deal(w1_w[b][:], w1_raw[b][:].rearrange("p (a c) -> p a c", a=PASSES))
+
+        def deal_scales(b):
+            by_pass = w1s_raw[:].rearrange("p (a c) -> p a c", a=PASSES)
+            deal(w1_s[b][:], by_pass[:, :, b * PASS_ROWS : (b + 1) * PASS_ROWS])
+
+        nc.vector.memset(tab_s[:].bitcast(I32)[:, :VECTOR_CLEARS], 0)
+        nc.gpsimd.memset(tab_s[:].bitcast(I32)[:, VECTOR_CLEARS:], 0)
+        nc.vector.memset(w1s_raw[:].bitcast(I32), 0)
+        nc.vector.memset(v_s[1][:].bitcast(I32), 0)
+
+        nc.gpsimd.dma_start(
+            gains[:].rearrange("p (b i) -> p b i", b=PASSES), gain.rearrange("(b p i) -> p b i", b=PASSES, i=PACK)
+        )
+        nc.sync.dma_start(idx[:], offs)
+        load_w1_words(0)
+        nc.sync.dma_start(tab_s[4:P:8, :].bitcast(I32), tab_scales[1].bitcast(I32))
+        for q in range(QUADRANTS):
+            nc.sync.dma_start(scale_rows(tab_s, q), tab_scales[0, PACK * q : PACK * (q + 1), :].bitcast(I32))
         load_table(0)
-        for q in range(4):
+        for q in range(QUADRANTS):
             nc.sync.dma_start(
-                w1s_raw[32 * q : 32 * q + 4, :].bitcast(I32).rearrange("r (a c) -> r a c", a=2),
-                w1_scales[:, 4 * q : 4 * q + 4, :].bitcast(I32).rearrange("a r c -> r a c"),
+                scale_rows(w1s_raw, q).rearrange("r (a c) -> r a c", a=PASSES),
+                w1_scales[:, PACK * q : PACK * (q + 1), :].bitcast(I32).rearrange("a r c -> r a c"),
             )
         nc.sync.dma_start(idx2[:], offs2)
         nc.sync.dma_start(idx3[:], offs3)
         load_table(1)
 
-        def deal(dst, src):
-            nc.vector.tensor_copy(
-                dst.rearrange("p (a i q) -> p a i q", a=2, i=PACK), src.rearrange("p a (q i) -> p a i q", i=PACK)
-            )
-
-        def deal_words(b):
-            deal(w1_w[b][:], w1_raw[b][:].rearrange("p (a c) -> p a c", a=2))
-
-        def deal_scales(b):
-            deal(w1_s[b][:], w1s_raw[:].rearrange("p (a c) -> p a c", a=2)[:, :, b * HALF : (b + 1) * HALF])
-
         nc.vector.tensor_copy(v_s[0][:], tab_s[:].indirect(idx[:]))
-        for r in range(4):
-            nc.sync.dma_start(v_s[1][r:P:32, :].bitcast(I32), v_s[0][4 + 8 * r : P : 32, :].bitcast(I32))
+        for r in range(PACK):
+            nc.sync.dma_start(
+                v_s[1][r:P:QUADRANT, :].bitcast(I32), v_s[0][4 + 8 * r : P : QUADRANT, :].bitcast(I32)
+            )
         deal_words(0)
         nc.vector.tensor_copy(v_w[0][:], tab_w[0][:].indirect(idx[:]))
         nc.sync.dma_start(wa[:], wga)
         nc.sync.dma_start(wb[:], wgb)
         load_w1_words(1)
         nc.sync.dma_start(
-            w2_raw[:].rearrange("p b j n -> p b (j n)"), w2.rearrange("(b p j) n -> p b (j n)", b=2, j=PACK)
+            w2_raw[:].rearrange("p b j n -> p b (j n)"), w2.rearrange("(b p j) n -> p b (j n)", b=PASSES, j=PACK)
         )
         deal_scales(0)
         deal_scales(1)
 
         banks = {}
         tanhs = {}
+        lefts = {}
+        spare = {}
 
         def first_product(s, j0, j1, a):
             if a == 0:
                 banks[s, j0] = hbanks.tile([P, j1 - j0], F32, name="h_bank")
             b, i = divmod(s, PACK)
             rows = slice((a * PACK + i) * P, (a * PACK + i + 1) * P)
-            cols = slice(j0, j1)
             nc.tensor.matmul_mx(
                 out=banks[s, j0][:],
                 lhsT=w1_w[b][:, rows].bitcast(FP4X4),
                 lhsT_scale=w1_s[b][:, rows],
-                rhs=v_w[a][:, cols].bitcast(FP8X4),
-                rhs_scale=v_s[a][:, cols],
+                rhs=v_w[a][:, j0:j1].bitcast(FP8X4),
+                rhs_scale=v_s[a][:, j0:j1],
                 start=(a == 0),
-                stop=(a == 1),
+                stop=(a == PASSES - 1),
             )
 
         def tanh(s, j0, j1):
-            if j0 == 0:
-                tanhs[s] = ring.tile([P, S], F32, name="tanh")
+            if s not in tanhs:
+                if s < VECTOR_GAINS:
+                    tanhs[s] = ring.tile([P, S], F32, name="tanh")
+                else:
+                    tanhs[s] = z_all[:, s - 1 : s + 1, :].rearrange("p u m -> p (u m)")
             nc.scalar.activation(tanhs[s][:, j0:j1], banks[s, j0][:], TANH)
 
-        def apply_gain(s, cols):
-            if s < VECTOR_GAINS:
-                nc.vector.tensor_scalar(h[s][:, cols], tanhs[s][:, cols], gains[:, s : s + 1], None, MULT)
-            else:
-                nc.scalar.activation(h[s][:, cols], tanhs[s][:, cols], COPY, scale=gains[:, s : s + 1])
+        def make_tanh(s, half):
+            for a in range(PASSES):
+                first_product(s, half * BANK, (half + 1) * BANK, a)
+            tanh(s, half * BANK, (half + 1) * BANK)
 
-        lefts = {}
+        def apply_gain(s, j0, j1):
+            if s < VECTOR_GAINS:
+                nc.vector.tensor_scalar(h[s][:, j0:j1], tanhs[s][:, j0:j1], gains[:, s : s + 1], None, MULT)
+            else:
+                nc.scalar.activation(h[s][:, j0:j1], tanhs[s][:, j0:j1], COPY, scale=gains[:, s : s + 1])
 
         def pick_left(s, m0, m1):
             lefts[s, m0] = ring.tile([P, m1 - m0], F32, name="left")
-            nc.vector.tensor_tensor(
-                lefts[s, m0][:], h[s][:].indirect(idx2[:, m0 // 16 : m1 // 16]), wab[:, m0:m1], MULT
-            )
+            offsets = idx2[:, m0 // LIST_ROWS : m1 // LIST_ROWS]
+            nc.vector.tensor_tensor(lefts[s, m0][:], h[s][:].indirect(offsets), wab[:, m0:m1], MULT)
 
-        def pick_right(s, m0, m1, l0):
-            nc.vector.tensor_tensor(
-                z[s // PACK][:, s % PACK, m0:m1],
-                h[s][:].indirect(idx3[:, m0 // 16 : m1 // 16]),
-                lefts[s, l0][:, m0 - l0 : m1 - l0],
-                MULT,
-            )
+        def pick_right(s, m0, m1, left_m0):
+            offsets = idx3[:, m0 // LIST_ROWS : m1 // LIST_ROWS]
+            left = lefts[s, left_m0][:, m0 - left_m0 : m1 - left_m0]
+            nc.vector.tensor_tensor(z[s // PACK][:, s % PACK, m0:m1], h[s][:].indirect(offsets), left, MULT)
 
         def weave(engine_copy, dst, src):
-            engine_copy(
-                dst.rearrange("p (m t) -> p m t", t=PACK), src.rearrange("p t m -> p m t")
-            )
+            engine_copy(dst.rearrange("p (m t) -> p m t", t=PACK), src.rearrange("p t m -> p m t"))
 
         def round_w2(b):
             nc.scalar.copy(
@@ -189,47 +209,39 @@ def tile_list_coral_neighbour_features_kernel(
 
         def quantize(words, scales, rounded, m0, m1):
             nc.vector.quantize_mx(
-                out=words[:, m0:m1].bitcast(FP8X4), scales=scales[:, m0:m1], in_=rounded
+                out=words[:, m0:m1].bitcast(FP8X4), scales=scales[:, m0:m1], in_=rounded[:, m0 * PACK : m1 * PACK]
             )
-
-        spare = {}
-
-        def y_sums(c, t):
-            if c == CHUNKS - 1 and t >= 2:
-                return spare[c][:, t - 2, :]
-            return y_bank[c][:, t, :]
 
         def second_product(c, b):
             cols = slice(c * CHUNK, (c + 1) * CHUNK)
-            split = c == CHUNKS - 1
-            if split and b == 0:
-                spare[c] = hbanks.tile([P, 2, CHUNK], F32, name="h_bank")
+            in_bank = PACK // 2 if c == LAST else PACK
+            if c == LAST and b == 0:
+                spare[c] = hbanks.tile([P, in_bank, CHUNK], F32, name="h_bank")
             for t in range(PACK):
                 rows = slice(t * P, (t + 1) * P)
                 nc.tensor.matmul_mx(
-                    out=y_sums(c, t),
+                    out=y_bank[c][:, t, :] if t < in_bank else spare[c][:, t - in_bank, :],
                     lhsT=w2_w[b][:, rows].bitcast(FP8X4),
                     lhsT_scale=w2_s[b][:, rows],
                     rhs=z_w[b][:, cols].bitcast(FP8X4),
                     rhs_scale=z_s[b][:, cols],
-                    start=(b == 0 and (t == 0 or (split and t == 2))),
-                    stop=(b == 1 and (t == PACK - 1 or (split and t == 1))),
+                    start=(b == 0 and t % in_bank == 0),
+                    stop=(b == PASSES - 1 and t % in_bank == in_bank - 1),
                 )
-
-        out_rows = out_0.rearrange("(p t) m -> p t m", t=PACK)
-        out_words = out_1[0].rearrange("p m t -> p (m t)").bitcast(I32)
 
         def round_z(c, engine_copy):
             m0, m1 = c * CHUNK, (c + 1) * CHUNK
             weave(engine_copy, z_bf[1][:, m0 * PACK : m1 * PACK], z[1][:, :, m0:m1])
 
-        def multiply(c):
-            m0, m1 = c * CHUNK, (c + 1) * CHUNK
-            quantize(z_w[1], z_s[1], z_bf[1][:, m0 * PACK : m1 * PACK], m0, m1)
+        def close_chunk(c):
+            quantize(z_w[1], z_s[1], z_bf[1], c * CHUNK, (c + 1) * CHUNK)
             second_product(c, 1)
 
         def drain(c):
             nc.scalar.copy(y[:, :, c * CHUNK : (c + 1) * CHUNK], y_bank[c][:])
+
+        out_rows = out_0.rearrange("(p t) m -> p t m", t=PACK)
+        out_words = out_1[0].rearrange("p m t -> p (m t)").bitcast(I32)
 
         def store_y(m0, m1):
             nc.sync.dma_start(out_rows[:, :, m0:m1], y[:, :, m0:m1])
@@ -237,88 +249,81 @@ def tile_list_coral_neighbour_features_kernel(
         def round_y(m0, m1, engine_copy):
             weave(engine_copy, y_bf[:, m0 * PACK : m1 * PACK], y[:, :, m0:m1])
 
-        def quantize_y(m0, m1):
-            quantize(y_w, y_s, y_bf[:, m0 * PACK : m1 * PACK], m0, m1)
-
-        def store_words(m0, m1):
+        def make_planes(m0, m1):
+            quantize(y_w, y_s, y_bf, m0, m1)
             nc.sync.dma_start(out_words[:, m0:m1], y_w[:, m0:m1].bitcast(I32))
 
-        early = [(0, 0, HALF), (1, 0, HALF), (0, HALF, 768), (0, 768, S)]
+        early = [(0, 0, BANK), (1, 0, BANK), (0, BANK, BANK + QUARTER), (0, BANK + QUARTER, S)]
         for piece in early:
             first_product(*piece, 0)
-        for half in range(2):
-            cols = slice(half * HALF, (half + 1) * HALF)
-            nc.vector.tensor_copy(v_w[1][:, cols], tab_w[1][:].indirect(idx[:, half * 32 : (half + 1) * 32]))
+        for j0 in range(0, S, BANK):
+            offsets = idx[:, j0 // LIST_ROWS : (j0 + BANK) // LIST_ROWS]
+            nc.vector.tensor_copy(v_w[1][:, j0 : j0 + BANK], tab_w[1][:].indirect(offsets))
         for piece in early:
             first_product(*piece, 1)
             tanh(*piece)
         nc.vector.tensor_tensor(wab[:], wa[:], wb[:], MULT)
-        for s, j0, j1 in early:
-            if s == 0:
-                apply_gain(s, slice(j0, j1))
+        for piece in early:
+            if piece[0] == 0:
+                apply_gain(*piece)
         pick_left(0, 0, M)
         deal_words(1)
-
-        def make_tanh(s, half):
-            for a in range(2):
-                first_product(s, half * HALF, (half + 1) * HALF, a)
-            tanh(s, half * HALF, (half + 1) * HALF)
-
         make_tanh(1, 1)
+
         for s in range(1, SLICES):
             if s + 1 < SLICES:
-                make_tanh(s + 1, 0)
-            apply_gain(s, slice(0, S))
-            if s == 5:
-                round_w2(0)
-            if s + 1 < SLICES:
                 make_tanh(s + 1, 1)
-            if s < 6:
+            apply_gain(s, 0, S)
+            if s + 1 < SLICES:
+                make_tanh(s + 1, 0)
+            if s < WHOLE_SLICES:
                 pick_left(s, 0, M)
                 pick_right(s - 1, 0, M, 0)
-            if s == 4:
-                weave(nc.vector.tensor_copy, z_bf[0][:], z[0][:])
-            if s == 5:
-                quantize(z_w[0], z_s[0], z_bf[0][:], 0, M)
-        round_w2(1)
-        pick_left(6, 0, 256)
-        pick_right(5, 0, M, 0)
-        quantize(w2_w[0], w2_s[0], w2_bf[0][:], 0, N)
+            if s == PACK:
+                weave(nc.vector.tensor_copy, z_bf[0][:], z[0])
+            if s == PACK + 1:
+                quantize(z_w[0], z_s[0], z_bf[0], 0, M)
+        for b in range(PASSES):
+            round_w2(b)
+
+        s6, s7 = WHOLE_SLICES, WHOLE_SLICES + 1
+        pick_left(s6, 0, MID)
+        pick_right(s6 - 1, 0, M, 0)
+        pick_left(s7, 0, MID)
+        pick_right(s6, 0, MID, 0)
+        quantize(w2_w[0], w2_s[0], w2_bf[0], 0, N)
         for c in range(CHUNKS):
             second_product(c, 0)
-        pick_left(7, 0, 256)
-        pick_right(6, 0, 256, 0)
-        pick_left(6, 256, M)
-        pick_right(7, 0, 256, 0)
+        pick_left(s6, MID, M)
+        pick_right(s7, 0, MID, 0)
         round_z(0, nc.scalar.copy)
         round_z(1, nc.scalar.copy)
-        pick_left(7, 256, M)
-        quantize(w2_w[1], w2_s[1], w2_bf[1][:], 0, N)
-        pick_right(6, 256, 384, 256)
-        multiply(0)
-        pick_right(7, 256, 384, 256)
+        pick_left(s7, MID, M)
+        quantize(w2_w[1], w2_s[1], w2_bf[1], 0, N)
+        pick_right(s6, MID, LAST_M0, MID)
+        close_chunk(0)
+        pick_right(s7, MID, LAST_M0, MID)
         round_z(2, nc.scalar.copy)
-        multiply(1)
-        pick_right(6, 384, M, 256)
-        pick_right(7, 384, M, 256)
+        close_chunk(1)
+        pick_right(s6, LAST_M0, M, MID)
+        pick_right(s7, LAST_M0, M, MID)
+
         drain(0)
-        multiply(2)
-        round_z(3, nc.vector.tensor_copy)
+        close_chunk(2)
+        round_z(LAST, nc.vector.tensor_copy)
         drain(1)
-        store_y(0, 256)
-        multiply(3)
-        round_y(0, 256, nc.vector.tensor_copy)
+        store_y(0, MID)
+        close_chunk(LAST)
+        round_y(0, MID, nc.vector.tensor_copy)
         drain(2)
-        store_y(256, 384)
-        quantize_y(0, 256)
-        store_words(0, 256)
-        nc.scalar.copy(y[:, 0:2, 384:M], y_bank[3][:, 0:2, :])
-        nc.vector.tensor_copy(y[:, 2:4, 384:M], spare[3][:])
-        store_y(384, M)
-        round_y(256, 384, nc.scalar.copy)
-        round_y(384, M, nc.vector.tensor_copy)
-        quantize_y(256, M)
-        store_words(256, M)
-        for q in range(4):
+        store_y(MID, LAST_M0)
+        make_planes(0, MID)
+        nc.scalar.copy(y[:, : PACK // 2, LAST_M0:], y_bank[LAST][:, : PACK // 2, :])
+        nc.vector.tensor_copy(y[:, PACK // 2 :, LAST_M0:], spare[LAST][:])
+        store_y(LAST_M0, M)
+        round_y(MID, LAST_M0, nc.scalar.copy)
+        round_y(LAST_M0, M, nc.vector.tensor_copy)
+        make_planes(MID, M)
+        for q in range(QUADRANTS):
             queue = nc.sync if q % 2 == 0 else nc.scalar
-            queue.dma_start(out_2[0, 4 * q : 4 * q + 4, :].bitcast(I32), y_s[32 * q : 32 * q + 4, :].bitcast(I32))
+            queue.dma_start(out_2[0, PACK * q : PACK * (q + 1), :].bitcast(I32), scale_rows(y_s, q))

from contextlib import ExitStack

import concourse.mybir as mybir

K, H, N, T, S, M = 1024, 1024, 512, 4096, 1024, 512
FLOPS = 2 * K * H * S + 2 * H * N * M

F32 = mybir.dt.float32
BF16 = mybir.dt.bfloat16
I32 = mybir.dt.int32
U32 = mybir.dt.uint32
U16 = mybir.dt.uint16
U8 = mybir.dt.uint8
FP8X4 = mybir.dt.float8_e4m3fn_x4
FP4X4 = mybir.dt.float4_e2m1fn_x4
MULT = mybir.AluOpType.mult
TANH = mybir.ActivationFunctionType.Tanh
COPY = mybir.ActivationFunctionType.Copy

P = 128
PACK = 4
PASSES = 2
PASS_ROWS = P * PACK
QUADRANT = 32
QUADRANTS = P // QUADRANT
LIST_ROWS = 16
SLICES = H // P
BANK = 512
QUARTER = BANK // 2
CHUNK = 128
CHUNKS = M // CHUNK
LAST = CHUNKS - 1
MID = M // 2
LAST_M0 = LAST * CHUNK
VECTOR_GAINS = 3
WHOLE_SLICES = SLICES - 2
VECTOR_CLEARS = 768
WA_AT, WB_AT, W1_AT, W2_AT, TABLE_STEP = 0, 2048, 4096, 8192, 24576


def tile_list_coral_neighbour_features_kernel(
    tc, tab_words, tab_scales, offs, offs2, offs3, w1_words, w1_scales, gain, wga, wgb, w2, out_0, out_1, out_2
):
    nc = tc.nc
    with ExitStack() as ctx:
        held = ctx.enter_context(tc.tile_pool(name="held", bufs=1))
        stage = ctx.enter_context(tc.tile_pool(name="stage", bufs=1))
        ring = ctx.enter_context(tc.tile_pool(name="ring", bufs=3))
        hbanks = ctx.enter_context(tc.psum_pool(name="hbanks", bufs=4))
        ybanks = ctx.enter_context(tc.psum_pool(name="ybanks", bufs=1))

        idx = held.tile([P, S // LIST_ROWS], U16, name="idx")
        idx2 = held.tile([P, M // LIST_ROWS], U16, name="idx2")
        idx3 = held.tile([P, M // LIST_ROWS], U16, name="idx3")
        tab_s = held.tile([P, T], U8, name="tab_s", align_bytes=64)
        tab_w = [
            stage.tile([P, T], U32, name=f"tab_w{a}", align_bytes=64, offset=TABLE_STEP * a) for a in range(PASSES)
        ]
        v_w = [held.tile([P, S], U32, name=f"v_w{a}", align_bytes=64) for a in range(PASSES)]
        v_s = [held.tile([P, S], U8, name=f"v_s{a}", align_bytes=64) for a in range(PASSES)]
        w1_raw = [
            held.tile([P, H], U16, name="w1_raw0", align_bytes=64),
            stage.tile([P, H], U16, name="w1_raw1", align_bytes=64, offset=W1_AT),
        ]
        w1s_raw = held.tile([P, PASSES * H], U8, name="w1s_raw", align_bytes=64)
        w1_w = [held.tile([P, H], U16, name=f"w1_w{b}", align_bytes=64) for b in range(PASSES)]
        w1_s = [held.tile([P, H], U8, name=f"w1_s{b}", align_bytes=64) for b in range(PASSES)]
        gains = held.tile([P, SLICES], F32, name="gains")
        wa = stage.tile([P, M], F32, name="wa", offset=WA_AT)
        wb = stage.tile([P, M], F32, name="wb", offset=WB_AT)
        wab = held.tile([P, M], F32, name="wab")
        w2_raw = stage.tile([P, PASSES, PACK, N], F32, name="w2_raw", offset=W2_AT)
        w2_bf = [held.tile([P, N * PACK], BF16, name=f"w2_bf{b}", align_bytes=64) for b in range(PASSES)]
        w2_w = [held.tile([P, N], U32, name=f"w2_w{b}", align_bytes=64) for b in range(PASSES)]
        w2_s = [held.tile([P, N], U8, name=f"w2_s{b}", align_bytes=64) for b in range(PASSES)]
        h = [held.tile([P, S], F32, name=f"h{s}", align_bytes=64) for s in range(SLICES)]
        z_all = held.tile([P, SLICES, M], F32, name="z_all", align_bytes=64)
        z = [z_all[:, b * PACK : (b + 1) * PACK, :] for b in range(PASSES)]
        z_bf = [held.tile([P, M * PACK], BF16, name=f"z_bf{b}", align_bytes=64) for b in range(PASSES)]
        z_w = [held.tile([P, M], U32, name=f"z_w{b}", align_bytes=64) for b in range(PASSES)]
        z_s = [held.tile([P, M], U8, name=f"z_s{b}", align_bytes=64) for b in range(PASSES)]
        y = held.tile([P, PACK, M], F32, name="y", align_bytes=64)
        y_bf = held.tile([P, M * PACK], BF16, name="y_bf", align_bytes=64)
        y_w = held.tile([P, M], U32, name="y_w", align_bytes=64)
        y_s = held.tile([P, M], U8, name="y_s", align_bytes=64)
        y_bank = [ybanks.tile([P, PACK, CHUNK], F32, name=f"y_bank{c}") for c in range(CHUNKS)]

        def scale_rows(tile, q):
            return tile[QUADRANT * q : QUADRANT * q + PACK, :].bitcast(I32)

        def load_w1_words(b):
            nc.sync.dma_start(
                w1_raw[b][:].bitcast(I32).rearrange("p (a c) -> p a c", a=PASSES),
                w1_words[:, :, b * H : (b + 1) * H].bitcast(I32).rearrange("a p c -> p a c"),
            )

        def load_table(a):
            nc.sync.dma_start(tab_w[a][:].bitcast(I32), tab_words[a].rearrange("p t i -> p (t i)").bitcast(I32))

        def deal(dst, src):
            nc.vector.tensor_copy(
                dst.rearrange("p (a i q) -> p a i q", a=PASSES, i=PACK),
                src.rearrange("p a (q i) -> p a i q", i=PACK),
            )

        def deal_words(b):
            deal(w1_w[b][:], w1_raw[b][:].rearrange("p (a c) -> p a c", a=PASSES))

        def deal_scales(b):
            by_pass = w1s_raw[:].rearrange("p (a c) -> p a c", a=PASSES)
            deal(w1_s[b][:], by_pass[:, :, b * PASS_ROWS : (b + 1) * PASS_ROWS])

        nc.vector.memset(tab_s[:].bitcast(I32)[:, :VECTOR_CLEARS], 0)
        nc.gpsimd.memset(tab_s[:].bitcast(I32)[:, VECTOR_CLEARS:], 0)
        nc.vector.memset(w1s_raw[:].bitcast(I32), 0)
        nc.vector.memset(v_s[1][:].bitcast(I32), 0)

        nc.gpsimd.dma_start(
            gains[:].rearrange("p (b i) -> p b i", b=PASSES), gain.rearrange("(b p i) -> p b i", b=PASSES, i=PACK)
        )
        nc.sync.dma_start(idx[:], offs)
        load_w1_words(0)
        nc.sync.dma_start(tab_s[4:P:8, :].bitcast(I32), tab_scales[1].bitcast(I32))
        for q in range(QUADRANTS):
            nc.sync.dma_start(scale_rows(tab_s, q), tab_scales[0, PACK * q : PACK * (q + 1), :].bitcast(I32))
        load_table(0)
        for q in range(QUADRANTS):
            nc.sync.dma_start(
                scale_rows(w1s_raw, q).rearrange("r (a c) -> r a c", a=PASSES),
                w1_scales[:, PACK * q : PACK * (q + 1), :].bitcast(I32).rearrange("a r c -> r a c"),
            )
        nc.sync.dma_start(idx2[:], offs2)
        nc.sync.dma_start(idx3[:], offs3)
        load_table(1)

        nc.vector.tensor_copy(v_s[0][:], tab_s[:].indirect(idx[:]))
        for r in range(PACK):
            nc.sync.dma_start(
                v_s[1][r:P:QUADRANT, :].bitcast(I32), v_s[0][4 + 8 * r : P : QUADRANT, :].bitcast(I32)
            )
        deal_words(0)
        nc.vector.tensor_copy(v_w[0][:], tab_w[0][:].indirect(idx[:]))
        nc.sync.dma_start(wa[:], wga)
        nc.sync.dma_start(wb[:], wgb)
        load_w1_words(1)
        nc.sync.dma_start(
            w2_raw[:].rearrange("p b j n -> p b (j n)"), w2.rearrange("(b p j) n -> p b (j n)", b=PASSES, j=PACK)
        )
        deal_scales(0)
        deal_scales(1)

        banks = {}
        tanhs = {}
        lefts = {}
        spare = {}

        def first_product(s, j0, j1, a):
            if a == 0:
                banks[s, j0] = hbanks.tile([P, j1 - j0], F32, name="h_bank")
            b, i = divmod(s, PACK)
            rows = slice((a * PACK + i) * P, (a * PACK + i + 1) * P)
            nc.tensor.matmul_mx(
                out=banks[s, j0][:],
                lhsT=w1_w[b][:, rows].bitcast(FP4X4),
                lhsT_scale=w1_s[b][:, rows],
                rhs=v_w[a][:, j0:j1].bitcast(FP8X4),
                rhs_scale=v_s[a][:, j0:j1],
                start=(a == 0),
                stop=(a == PASSES - 1),
            )

        def tanh(s, j0, j1):
            if s not in tanhs:
                if s < VECTOR_GAINS:
                    tanhs[s] = ring.tile([P, S], F32, name="tanh")
                else:
                    tanhs[s] = z_all[:, s - 1 : s + 1, :].rearrange("p u m -> p (u m)")
            nc.scalar.activation(tanhs[s][:, j0:j1], banks[s, j0][:], TANH)

        def make_tanh(s, half):
            for a in range(PASSES):
                first_product(s, half * BANK, (half + 1) * BANK, a)
            tanh(s, half * BANK, (half + 1) * BANK)

        def apply_gain(s, j0, j1):
            if s < VECTOR_GAINS:
                nc.vector.tensor_scalar(h[s][:, j0:j1], tanhs[s][:, j0:j1], gains[:, s : s + 1], None, MULT)
            else:
                nc.scalar.activation(h[s][:, j0:j1], tanhs[s][:, j0:j1], COPY, scale=gains[:, s : s + 1])

        def pick_left(s, m0, m1):
            lefts[s, m0] = ring.tile([P, m1 - m0], F32, name="left")
            offsets = idx2[:, m0 // LIST_ROWS : m1 // LIST_ROWS]
            nc.vector.tensor_tensor(lefts[s, m0][:], h[s][:].indirect(offsets), wab[:, m0:m1], MULT)

        def pick_right(s, m0, m1, left_m0):
            offsets = idx3[:, m0 // LIST_ROWS : m1 // LIST_ROWS]
            left = lefts[s, left_m0][:, m0 - left_m0 : m1 - left_m0]
            nc.vector.tensor_tensor(z[s // PACK][:, s % PACK, m0:m1], h[s][:].indirect(offsets), left, MULT)

        def weave(engine_copy, dst, src):
            engine_copy(dst.rearrange("p (m t) -> p m t", t=PACK), src.rearrange("p t m -> p m t"))

        def round_w2(b):
            nc.scalar.copy(
                w2_bf[b][:].rearrange("p (t q j) -> p q t j", t=PACK, j=PACK),
                w2_raw[:, b].rearrange("p j (q t) -> p q t j", t=PACK),
            )

        def quantize(words, scales, rounded, m0, m1):
            nc.vector.quantize_mx(
                out=words[:, m0:m1].bitcast(FP8X4), scales=scales[:, m0:m1], in_=rounded[:, m0 * PACK : m1 * PACK]
            )

        def second_product(c, b):
            cols = slice(c * CHUNK, (c + 1) * CHUNK)
            in_bank = PACK // 2 if c == LAST else PACK
            if c == LAST and b == 0:
                spare[c] = hbanks.tile([P, in_bank, CHUNK], F32, name="h_bank")
            for t in range(PACK):
                rows = slice(t * P, (t + 1) * P)
                nc.tensor.matmul_mx(
                    out=y_bank[c][:, t, :] if t < in_bank else spare[c][:, t - in_bank, :],
                    lhsT=w2_w[b][:, rows].bitcast(FP8X4),
                    lhsT_scale=w2_s[b][:, rows],
                    rhs=z_w[b][:, cols].bitcast(FP8X4),
                    rhs_scale=z_s[b][:, cols],
                    start=(b == 0 and t % in_bank == 0),
                    stop=(b == PASSES - 1 and t % in_bank == in_bank - 1),
                )

        def round_z(c, engine_copy):
            m0, m1 = c * CHUNK, (c + 1) * CHUNK
            weave(engine_copy, z_bf[1][:, m0 * PACK : m1 * PACK], z[1][:, :, m0:m1])

        def close_chunk(c):
            quantize(z_w[1], z_s[1], z_bf[1], c * CHUNK, (c + 1) * CHUNK)
            second_product(c, 1)

        def drain(c):
            nc.scalar.copy(y[:, :, c * CHUNK : (c + 1) * CHUNK], y_bank[c][:])

        out_rows = out_0.rearrange("(p t) m -> p t m", t=PACK)
        out_words = out_1[0].rearrange("p m t -> p (m t)").bitcast(I32)

        def store_y(m0, m1):
            nc.sync.dma_start(out_rows[:, :, m0:m1], y[:, :, m0:m1])

        def round_y(m0, m1, engine_copy):
            weave(engine_copy, y_bf[:, m0 * PACK : m1 * PACK], y[:, :, m0:m1])

        def make_planes(m0, m1):
            quantize(y_w, y_s, y_bf, m0, m1)
            nc.sync.dma_start(out_words[:, m0:m1], y_w[:, m0:m1].bitcast(I32))

        early = [(0, 0, BANK), (1, 0, BANK), (0, BANK, BANK + QUARTER), (0, BANK + QUARTER, S)]
        for piece in early:
            first_product(*piece, 0)
        for j0 in range(0, S, BANK):
            offsets = idx[:, j0 // LIST_ROWS : (j0 + BANK) // LIST_ROWS]
            nc.vector.tensor_copy(v_w[1][:, j0 : j0 + BANK], tab_w[1][:].indirect(offsets))
        for piece in early:
            first_product(*piece, 1)
            tanh(*piece)
        nc.vector.tensor_tensor(wab[:], wa[:], wb[:], MULT)
        for piece in early:
            if piece[0] == 0:
                apply_gain(*piece)
        pick_left(0, 0, M)
        deal_words(1)
        make_tanh(1, 1)

        for s in range(1, SLICES):
            if s + 1 < SLICES:
                make_tanh(s + 1, 1)
            apply_gain(s, 0, S)
            if s + 1 < SLICES:
                make_tanh(s + 1, 0)
            if s < WHOLE_SLICES:
                pick_left(s, 0, M)
                pick_right(s - 1, 0, M, 0)
            if s == PACK:
                weave(nc.vector.tensor_copy, z_bf[0][:], z[0])
            if s == PACK + 1:
                quantize(z_w[0], z_s[0], z_bf[0], 0, M)
        for b in range(PASSES):
            round_w2(b)

        s6, s7 = WHOLE_SLICES, WHOLE_SLICES + 1
        pick_left(s6, 0, MID)
        pick_right(s6 - 1, 0, M, 0)
        pick_left(s7, 0, MID)
        pick_right(s6, 0, MID, 0)
        quantize(w2_w[0], w2_s[0], w2_bf[0], 0, N)
        for c in range(CHUNKS):
            second_product(c, 0)
        pick_left(s6, MID, M)
        pick_right(s7, 0, MID, 0)
        round_z(0, nc.scalar.copy)
        round_z(1, nc.scalar.copy)
        pick_left(s7, MID, M)
        quantize(w2_w[1], w2_s[1], w2_bf[1], 0, N)
        pick_right(s6, MID, LAST_M0, MID)
        close_chunk(0)
        pick_right(s7, MID, LAST_M0, MID)
        round_z(2, nc.scalar.copy)
        close_chunk(1)
        pick_right(s6, LAST_M0, M, MID)
        pick_right(s7, LAST_M0, M, MID)

        drain(0)
        close_chunk(2)
        round_z(LAST, nc.vector.tensor_copy)
        drain(1)
        store_y(0, MID)
        close_chunk(LAST)
        round_y(0, MID, nc.vector.tensor_copy)
        drain(2)
        store_y(MID, LAST_M0)
        make_planes(0, MID)
        nc.scalar.copy(y[:, : PACK // 2, LAST_M0:], y_bank[LAST][:, : PACK // 2, :])
        nc.vector.tensor_copy(y[:, PACK // 2 :, LAST_M0:], spare[LAST][:])
        store_y(LAST_M0, M)
        round_y(MID, LAST_M0, nc.scalar.copy)
        round_y(LAST_M0, M, nc.vector.tensor_copy)
        make_planes(MID, M)
        for q in range(QUADRANTS):
            queue = nc.sync if q % 2 == 0 else nc.scalar
            queue.dma_start(out_2[0, PACK * q : PACK * (q + 1), :].bitcast(I32), scale_rows(y_s, q))
